import numpy as np, ml_dtypes
CORES = [2,3,42,43,82,83,122,123]
N = 8
F = 32
def setup_inputs(rng):
    x = (rng.standard_normal((N, 128, 128), dtype=np.float32) / 11).astype(ml_dtypes.bfloat16)
    w = rng.standard_normal((128, F), dtype=np.float32).astype(ml_dtypes.bfloat16)
    return {"x": x, "xt": x.transpose(0, 2, 1).copy(), "w": np.broadcast_to(w, (N, 128, F)).copy()}
def setup_inputs_big(rng):
    d = setup_inputs(rng)
    for k in ("x", "xt", "w"): d[k] = (d[k].astype(np.float32) * 1024.0).astype(d[k].dtype)
    return d
def setup_inputs_small(rng):
    d = setup_inputs(rng)
    for k in ("x", "xt", "w"): d[k] = (d[k].astype(np.float32) * (1 / 1024.0)).astype(d[k].dtype)
    return d
def setup_inputs_apart(rng):
    d = setup_inputs(rng)
    f = (10.0 ** rng.permutation(np.linspace(-1.5, 1.5, N))).astype(np.float32).reshape(N, 1, 1)
    for k in ("x", "xt"): d[k] = (d[k].astype(np.float32) * f).astype(d[k].dtype)
    return d
def reference(x, xt, w):
    X, XT, W = x.astype(np.float64), xt.astype(np.float64), w.astype(np.float64)
    s = sum(X[j].T @ (XT[j].T @ W[j]) for j in range(N)).astype(ml_dtypes.bfloat16)
    return {"y": np.broadcast_to(s, (N,) + s.shape)}

@@ -1,0 +1,84 @@
+from concourse.bass import DstId, RemoteDMATransfer
+
+NR = 8
+F = 32
+ENGINES = 4
+
+SCRATCH = {
+    "xs": ("sbuf", [128, 128], "bfloat16"),
+    "ws": ("sbuf", [128, F], "bfloat16"),
+    "gs": ("sbuf", [128, 128], "bfloat16"),
+    "pt": ("sbuf", [128, 128], "bfloat16"),
+    "seed": ("sbuf", [128, 1024], "bfloat16"),
+    "sel": ("sbuf", [128, 2 * F], "bfloat16"),
+    "z": ("sbuf", [128, 256], "bfloat16"),
+    "ys": ("sbuf", [128, F], "bfloat16"),
+    "land": ("dram", [NR, 128, F], "bfloat16"),
+    "gp": ("psum", [128, 512], "float32"),
+    "pp": ("psum", [128, 512], "float32"),
+    "yp": ("psum", [128, 512], "float32"),
+}
+SEMAPHORES = ["ldx", "ldw", "fill", "selr", "mm", "cp", "put", "arr", "sent", "got", "st"]
+
+
+def rank_program(g, core, T, topo):
+    rank = T.rank_of(core)
+    if rank is None:
+        return
+    S = T.sem
+    others = [c for c in T.cores if c != core]
+    for d in others:
+        assert topo.may_write(core, d)
+    common = topo.mask(core, others[0])
+    for d in others:
+        common &= topo.mask(core, d)
+    bits = [b for b in range(common.bit_length()) if (common >> b) & 1]
+    step = max(1, len(bits) // ENGINES)
+    chosen = bits[::step][:ENGINES]
+    mask = sum(1 << b for b in chosen)
+
+    g.sync.dma_start(T.xs[:], T.x[:]).then_inc(S.ldx, 16)
+    g.scalar.dma_start(T.ws[:], T.w[:]).then_inc(S.ldw, 16)
+
+    g.vector.memset(T.seed[0:8, :], 0.0).then_inc(S.fill, 1)
+    g.vector.wait_ge(S.fill, 1)
+    g.vector.memset(T.seed[0:8, 0:1024:33], 1.0).then_inc(S.fill, 1)
+    g.scalar.wait_ge(S.fill, 2)
+    g.scalar.dma_start(T.sel[:], T.seed[0:8, :]).then_inc(S.selr, 16)
+
+    g.tensor.wait_ge(S.ldx, 16)
+    g.tensor.matmul(T.gp[:, 0:128], T.xs[:], T.xs[:], start=True, stop=True).then_inc(S.mm, 1)
+    g.vector.wait_ge(S.mm, 1)
+    g.vector.tensor_copy(T.gs[:], T.gp[:, 0:128]).then_inc(S.cp, 1)
+    g.tensor.wait_ge(S.cp, 1)
+    g.tensor.wait_ge(S.ldw, 16)
+    g.tensor.matmul(T.pp[0:F, 0:128], T.ws[:], T.gs[:], start=True, stop=True).then_inc(S.mm, 1)
+    g.vector.wait_ge(S.mm, 2)
+    g.vector.tensor_copy(T.pt[0:F, :], T.pp[0:F, 0:128]).then_inc(S.cp, 1)
+    g.sync.wait_ge(S.cp, 2)
+    g.sync.dma_start(T.land[rank], T.pt[0:F, :]).then_inc(S.put, 16)
+
+    g.wait_ge(S.put, 16)
+    ids = []
+    for d in others:
+        rid, pid, _ = topo.addr(d)
+        ids.append(DstId(rid=rid, pnc=pid))
+    g.remote_dma_fused(
+        [RemoteDMATransfer(dst_ids=ids, dma_engine_mask=mask, remote_sem=S.arr,
+                           srcs=[T.land[rank]], dsts=[T.land[rank] for _ in others])],
+        local_sem=S.sent)
+
+    g.sync.wait_ge(S.put, 16)
+    g.sync.wait_ge(S.arr, len(others) * len(chosen))
+    g.sync.dma_start(T.z[:], T.land[:]).then_inc(S.got, 16)
+    g.tensor.wait_ge(S.selr, 16)
+    g.tensor.wait_ge(S.got, 16)
+    g.tensor.matmul(T.yp[:, 0:F], T.z[:, 0:128], T.sel[:, 0:F], start=True, stop=False)
+    g.tensor.matmul(T.yp[:, 0:F], T.z[:, 128:256], T.sel[:, F:2 * F], start=False, stop=True).then_inc(S.mm, 1)
+
+    g.vector.wait_ge(S.mm, 3)
+    g.vector.tensor_copy(T.ys[:], T.yp[:, 0:F]).then_inc(S.cp, 1)
+    g.sync.wait_ge(S.cp, 3)
+    g.sync.dma_start(T.y[:], T.ys[:]).then_inc(S.st, 16)
+    g.sync.wait_ge(S.st, 16)
+    g.wait_ge(S.sent, len(chosen))

@@ -1,24 +1,20 @@
 from concourse.bass import DstId, RemoteDMATransfer
+from concourse.mybir import AluOpType
 
 NR = 8
 F = 32
-ENGINES = 4
 
 SCRATCH = {
     "xs": ("sbuf", [128, 128], "bfloat16"),
     "ws": ("sbuf", [128, F], "bfloat16"),
     "gs": ("sbuf", [128, 128], "bfloat16"),
-    "pt": ("sbuf", [128, 128], "bfloat16"),
-    "seed": ("sbuf", [128, 1024], "bfloat16"),
-    "sel": ("sbuf", [128, 2 * F], "bfloat16"),
-    "z": ("sbuf", [128, 256], "bfloat16"),
+    "land": ("sbuf", [128, NR * F], "bfloat16"),
+    "acc": ("sbuf", [128, NR * F], "float32"),
     "ys": ("sbuf", [128, F], "bfloat16"),
-    "land": ("dram", [NR, 128, F], "bfloat16"),
     "gp": ("psum", [128, 512], "float32"),
     "pp": ("psum", [128, 512], "float32"),
-    "yp": ("psum", [128, 512], "float32"),
 }
-SEMAPHORES = ["ldx", "ldw", "fill", "selr", "mm", "cp", "put", "arr", "sent", "got", "st"]
+SEMAPHORES = ["ldx", "ldw", "mm", "cp", "sent", "vs", "st"] + ["a%d" % j for j in range(NR)]
 
 
 def rank_program(g, core, T, topo):
@@ -26,25 +22,17 @@ def rank_program(g, core, T, topo):
     if rank is None:
         return
     S = T.sem
-    others = [c for c in T.cores if c != core]
-    for d in others:
+    n = len(T.cores)
+    dests = [T.cores[(rank + s) % n] for s in range(1, n)]
+    senders = [(rank - s) % n for s in range(1, n)]
+    mask = topo.mask(core, dests[0])
+    for d in dests:
         assert topo.may_write(core, d)
-    common = topo.mask(core, others[0])
-    for d in others:
-        common &= topo.mask(core, d)
-    bits = [b for b in range(common.bit_length()) if (common >> b) & 1]
-    step = max(1, len(bits) // ENGINES)
-    chosen = bits[::step][:ENGINES]
-    mask = sum(1 << b for b in chosen)
+        mask &= topo.mask(core, d)
+    ne = bin(mask).count("1")
 
     g.sync.dma_start(T.xs[:], T.x[:]).then_inc(S.ldx, 16)
     g.scalar.dma_start(T.ws[:], T.w[:]).then_inc(S.ldw, 16)
-
-    g.vector.memset(T.seed[0:8, :], 0.0).then_inc(S.fill, 1)
-    g.vector.wait_ge(S.fill, 1)
-    g.vector.memset(T.seed[0:8, 0:1024:33], 1.0).then_inc(S.fill, 1)
-    g.scalar.wait_ge(S.fill, 2)
-    g.scalar.dma_start(T.sel[:], T.seed[0:8, :]).then_inc(S.selr, 16)
 
     g.tensor.wait_ge(S.ldx, 16)
     g.tensor.matmul(T.gp[:, 0:128], T.xs[:], T.xs[:], start=True, stop=True).then_inc(S.mm, 1)
@@ -52,33 +40,32 @@ def rank_program(g, core, T, topo):
     g.vector.tensor_copy(T.gs[:], T.gp[:, 0:128]).then_inc(S.cp, 1)
     g.tensor.wait_ge(S.cp, 1)
     g.tensor.wait_ge(S.ldw, 16)
-    g.tensor.matmul(T.pp[0:F, 0:128], T.ws[:], T.gs[:], start=True, stop=True).then_inc(S.mm, 1)
+    g.tensor.matmul(T.pp[:, 0:F], T.gs[:], T.ws[:], start=True, stop=True).then_inc(S.mm, 1)
+    own = T.land[:, rank * F:(rank + 1) * F]
     g.vector.wait_ge(S.mm, 2)
-    g.vector.tensor_copy(T.pt[0:F, :], T.pp[0:F, 0:128]).then_inc(S.cp, 1)
-    g.sync.wait_ge(S.cp, 2)
-    g.sync.dma_start(T.land[rank], T.pt[0:F, :]).then_inc(S.put, 16)
+    g.vector.tensor_copy(own, T.pp[:, 0:F]).then_inc(S.cp, 1)
 
-    g.wait_ge(S.put, 16)
+    g.wait_ge(S.cp, 2)
     ids = []
-    for d in others:
+    for d in dests:
         rid, pid, _ = topo.addr(d)
         ids.append(DstId(rid=rid, pnc=pid))
     g.remote_dma_fused(
-        [RemoteDMATransfer(dst_ids=ids, dma_engine_mask=mask, remote_sem=S.arr,
-                           srcs=[T.land[rank]], dsts=[T.land[rank] for _ in others])],
+        [RemoteDMATransfer(dst_ids=ids, dma_engine_mask=mask, remote_sem=S["a%d" % rank],
+                           srcs=[own], dsts=[own for _ in dests])],
         local_sem=S.sent)
 
-    g.sync.wait_ge(S.put, 16)
-    g.sync.wait_ge(S.arr, len(others) * len(chosen))
-    g.sync.dma_start(T.z[:], T.land[:]).then_inc(S.got, 16)
-    g.tensor.wait_ge(S.selr, 16)
-    g.tensor.wait_ge(S.got, 16)
-    g.tensor.matmul(T.yp[:, 0:F], T.z[:, 0:128], T.sel[:, 0:F], start=True, stop=False)
-    g.tensor.matmul(T.yp[:, 0:F], T.z[:, 128:256], T.sel[:, F:2 * F], start=False, stop=True).then_inc(S.mm, 1)
+    prev = T.pp[:, 0:F]
+    for k, j in enumerate(senders):
+        last = k == len(senders) - 1
+        out = T.ys[:] if last else T.acc[:, k * F:(k + 1) * F]
+        g.vector.wait_ge(S["a%d" % j], ne)
+        if k:
+            g.vector.wait_ge(S.vs, k)
+        g.vector.tensor_tensor(out, prev, T.land[:, j * F:(j + 1) * F], AluOpType.add).then_inc(S.vs, 1)
+        prev = out
 
-    g.vector.wait_ge(S.mm, 3)
-    g.vector.tensor_copy(T.ys[:], T.yp[:, 0:F]).then_inc(S.cp, 1)
-    g.sync.wait_ge(S.cp, 3)
+    g.sync.wait_ge(S.vs, len(senders))
     g.sync.dma_start(T.y[:], T.ys[:]).then_inc(S.st, 16)
     g.sync.wait_ge(S.st, 16)
-    g.wait_ge(S.sent, len(chosen))
+    g.wait_ge(S.sent, ne)

@@ -6,15 +6,19 @@ F = 32
 
 SCRATCH = {
     "xs": ("sbuf", [128, 128], "bfloat16"),
+    "xq": ("sbuf", [128, 128], "bfloat16"),
     "ws": ("sbuf", [128, F], "bfloat16"),
     "gs": ("sbuf", [128, 128], "bfloat16"),
+    "gqs": ("sbuf", [128, 128], "bfloat16"),
     "land": ("sbuf", [128, NR * F], "bfloat16"),
     "acc": ("sbuf", [128, NR * F], "float32"),
     "ys": ("sbuf", [128, F], "bfloat16"),
     "gp": ("psum", [128, 512], "float32"),
     "pp": ("psum", [128, 512], "float32"),
+    "gq": ("psum", [128, 512], "float32"),
+    "qq": ("psum", [128, 512], "float32"),
 }
-SEMAPHORES = ["ldx", "ldw", "mm", "cp", "sent", "vs", "st"] + ["a%d" % j for j in range(NR)]
+SEMAPHORES = ["ldx", "ldw", "mm", "cp", "xin", "sent", "vs", "st"] + ["a%d" % j for j in range(NR)]
 
 
 def rank_program(g, core, T, topo):
@@ -23,16 +27,23 @@ def rank_program(g, core, T, topo):
         return
     S = T.sem
     n = len(T.cores)
-    dests = [T.cores[(rank + s) % n] for s in range(1, n)]
-    senders = [(rank - s) % n for s in range(1, n)]
-    mask = topo.mask(core, dests[0])
-    for d in dests:
+    near = [c for c in T.cores if c != core and topo.chip(c) == topo.chip(core)]
+    assert len(near) == 1
+    partner = near[0]
+    dests = [T.cores[(rank + s) % n] for s in range(1, n) if T.cores[(rank + s) % n] != partner]
+    senders = [(rank - s) % n for s in range(1, n) if T.cores[(rank - s) % n] != partner]
+    mask = topo.mask(core, partner)
+    for d in dests + [partner]:
         assert topo.may_write(core, d)
         mask &= topo.mask(core, d)
     ne = bin(mask).count("1")
 
     g.sync.dma_start(T.xs[:], T.x[:]).then_inc(S.ldx, 16)
     g.scalar.dma_start(T.ws[:], T.w[:]).then_inc(S.ldw, 16)
+
+    g.wait_ge(S.ldx, 16)
+    rid, pid, _ = topo.addr(partner)
+    g.remote_dma(T.xq[:], T.xs[:], remote_sem=S.xin, local_sem=S.sent, pid=pid, routing_id=rid, dma_engine_mask=mask)
 
     g.tensor.wait_ge(S.ldx, 16)
     g.tensor.matmul(T.gp[:, 0:128], T.xs[:], T.xs[:], start=True, stop=True).then_inc(S.mm, 1)
@@ -55,17 +66,34 @@ def rank_program(g, core, T, topo):
                            srcs=[own], dsts=[own for _ in dests])],
         local_sem=S.sent)
 
-    prev = T.pp[:, 0:F]
-    for k, j in enumerate(senders):
-        last = k == len(senders) - 1
-        out = T.ys[:] if last else T.acc[:, k * F:(k + 1) * F]
-        g.vector.wait_ge(S["a%d" % j], ne)
+    g.tensor.matmul(T.qq[:, 0:F], T.gs[:], T.ws[:], start=True, stop=False)
+    g.tensor.wait_ge(S.xin, ne)
+    g.tensor.matmul(T.gq[:, 0:128], T.xq[:], T.xq[:], start=True, stop=True).then_inc(S.mm, 1)
+    g.vector.wait_ge(S.mm, 3)
+    g.vector.tensor_copy(T.gqs[:], T.gq[:, 0:128]).then_inc(S.cp, 1)
+    g.tensor.wait_ge(S.cp, 3)
+    g.tensor.matmul(T.qq[:, 0:F], T.gqs[:], T.ws[:], start=False, stop=True).then_inc(S.mm, 1)
+
+    def block(j):
+        return T.land[:, j * F:(j + 1) * F]
+
+    terms = [("b", j) for j in senders[1:3]] + [("q", None)] + [("b", j) for j in senders[3:]]
+    g.vector.wait_ge(S["a%d" % senders[0]], ne)
+    prev = block(senders[0])
+    for k, (kind, j) in enumerate(terms):
+        out = T.ys[:] if k == len(terms) - 1 else T.acc[:, k * F:(k + 1) * F]
+        if kind == "b":
+            g.vector.wait_ge(S["a%d" % j], ne)
+            other = block(j)
+        else:
+            g.vector.wait_ge(S.mm, 4)
+            other = T.qq[:, 0:F]
         if k:
             g.vector.wait_ge(S.vs, k)
-        g.vector.tensor_tensor(out, prev, T.land[:, j * F:(j + 1) * F], AluOpType.add).then_inc(S.vs, 1)
+        g.vector.tensor_tensor(out, other, prev, AluOpType.add).then_inc(S.vs, 1)
         prev = out
 
-    g.sync.wait_ge(S.vs, len(senders))
+    g.sync.wait_ge(S.vs, len(terms))
     g.sync.dma_start(T.y[:], T.ys[:]).then_inc(S.st, 16)
     g.sync.wait_ge(S.st, 16)
-    g.wait_ge(S.sent, ne)
+    g.wait_ge(S.sent, 2 * ne)

@@ -1,5 +1,4 @@
 from concourse.bass import DstId, RemoteDMATransfer
-from concourse.mybir import AluOpType
 
 NR = 8
 F = 32
@@ -11,14 +10,16 @@ SCRATCH = {
     "gs": ("sbuf", [128, 128], "bfloat16"),
     "gqs": ("sbuf", [128, 128], "bfloat16"),
     "land": ("sbuf", [128, NR * F], "bfloat16"),
-    "acc": ("sbuf", [128, NR * F], "float32"),
+    "seed": ("sbuf", [128, 129], "bfloat16"),
+    "skew": ("dram", [129, 128], "bfloat16"),
+    "ident": ("sbuf", [128, 128], "bfloat16"),
     "ys": ("sbuf", [128, F], "bfloat16"),
     "gp": ("psum", [128, 512], "float32"),
     "pp": ("psum", [128, 512], "float32"),
     "gq": ("psum", [128, 512], "float32"),
     "qq": ("psum", [128, 512], "float32"),
 }
-SEMAPHORES = ["ldx", "ldw", "mm", "cp", "xin", "sent", "vs", "st"] + ["a%d" % j for j in range(NR)]
+SEMAPHORES = ["ldx", "ldw", "fill", "sk", "idr", "mm", "cp", "xin", "sent", "st"] + ["a%d" % j for j in range(NR)]
 
 
 def rank_program(g, core, T, topo):
@@ -26,12 +27,24 @@ def rank_program(g, core, T, topo):
     if rank is None:
         return
     S = T.sem
-    n = len(T.cores)
-    near = [c for c in T.cores if c != core and topo.chip(c) == topo.chip(core)]
-    assert len(near) == 1
-    partner = near[0]
-    dests = [T.cores[(rank + s) % n] for s in range(1, n) if T.cores[(rank + s) % n] != partner]
-    senders = [(rank - s) % n for s in range(1, n) if T.cores[(rank - s) % n] != partner]
+    chips = []
+    for c in T.cores:
+        if topo.chip(c) not in chips:
+            chips.append(topo.chip(c))
+    members = [[c for c in T.cores if topo.chip(c) == ch] for ch in chips]
+    nc, m = len(chips), len(members[0])
+    assert m == 2 and all(len(x) == m for x in members)
+    a = chips.index(topo.chip(core))
+    b = members[a].index(core)
+    partner = members[a][1 - b]
+
+    def hops(d):
+        return max(1 if topo.mates(chips[i], chips[(i + d) % nc]) or topo.same_plane(chips[i], chips[(i + d) % nc])
+                   else 2 for i in range(nc))
+
+    steps = [(d, e) for d in sorted(range(1, nc), key=lambda d: -hops(d)) for e in range(m)]
+    dests = [members[(a + d) % nc][(b + e) % m] for d, e in steps]
+    senders = [T.rank_of(members[(a - d) % nc][(b - e) % m]) for d, e in steps]
     mask = topo.mask(core, partner)
     for d in dests + [partner]:
         assert topo.may_write(core, d)
@@ -39,7 +52,15 @@ def rank_program(g, core, T, topo):
     ne = bin(mask).count("1")
 
     g.sync.dma_start(T.xs[:], T.x[:]).then_inc(S.ldx, 16)
-    g.scalar.dma_start(T.ws[:], T.w[:]).then_inc(S.ldw, 16)
+    g.sync.dma_start(T.ws[:], T.w[:]).then_inc(S.ldw, 16)
+
+    g.vector.memset(T.seed[:], 0.0).then_inc(S.fill, 1)
+    g.vector.wait_ge(S.fill, 1)
+    g.vector.memset(T.seed[:, 0:1], 1.0).then_inc(S.fill, 1)
+    g.scalar.wait_ge(S.fill, 2)
+    g.scalar.dma_start(T.skew[:], T.seed[:]).then_inc(S.sk, 16)
+    g.scalar.wait_ge(S.sk, 16)
+    g.scalar.dma_start(T.ident[:], T.skew[0:128, :]).then_inc(S.idr, 16)
 
     g.wait_ge(S.ldx, 16)
     rid, pid, _ = topo.addr(partner)
@@ -66,34 +87,25 @@ def rank_program(g, core, T, topo):
                            srcs=[own], dsts=[own for _ in dests])],
         local_sem=S.sent)
 
-    g.tensor.matmul(T.qq[:, 0:F], T.gs[:], T.ws[:], start=True, stop=False)
+    yp = T.qq[:, 0:F]
+    g.tensor.matmul(yp, T.gs[:], T.ws[:], start=True, stop=False)
     g.tensor.wait_ge(S.xin, ne)
     g.tensor.matmul(T.gq[:, 0:128], T.xq[:], T.xq[:], start=True, stop=True).then_inc(S.mm, 1)
     g.vector.wait_ge(S.mm, 3)
     g.vector.tensor_copy(T.gqs[:], T.gq[:, 0:128]).then_inc(S.cp, 1)
-    g.tensor.wait_ge(S.cp, 3)
-    g.tensor.matmul(T.qq[:, 0:F], T.gqs[:], T.ws[:], start=False, stop=True).then_inc(S.mm, 1)
+    g.tensor.wait_ge(S.idr, 16)
+    late = len(senders) - 2
+    for k, j in enumerate(senders):
+        if k == late:
+            g.tensor.wait_ge(S.cp, 3)
+            g.tensor.matmul(yp, T.gqs[:], T.ws[:], start=False, stop=False)
+        g.tensor.wait_ge(S["a%d" % j], ne)
+        mmk = g.tensor.matmul(yp, T.ident[:], T.land[:, j * F:(j + 1) * F], start=False, stop=(k == len(senders) - 1))
+    mmk.then_inc(S.mm, 1)
 
-    def block(j):
-        return T.land[:, j * F:(j + 1) * F]
-
-    terms = [("b", j) for j in senders[1:3]] + [("q", None)] + [("b", j) for j in senders[3:]]
-    g.vector.wait_ge(S["a%d" % senders[0]], ne)
-    prev = block(senders[0])
-    for k, (kind, j) in enumerate(terms):
-        out = T.ys[:] if k == len(terms) - 1 else T.acc[:, k * F:(k + 1) * F]
-        if kind == "b":
-            g.vector.wait_ge(S["a%d" % j], ne)
-            other = block(j)
-        else:
-            g.vector.wait_ge(S.mm, 4)
-            other = T.qq[:, 0:F]
-        if k:
-            g.vector.wait_ge(S.vs, k)
-        g.vector.tensor_tensor(out, other, prev, AluOpType.add).then_inc(S.vs, 1)
-        prev = out
-
-    g.sync.wait_ge(S.vs, len(terms))
+    g.vector.wait_ge(S.mm, 4)
+    g.vector.tensor_copy(T.ys[:], yp).then_inc(S.cp, 1)
+    g.sync.wait_ge(S.cp, 4)
     g.sync.dma_start(T.y[:], T.ys[:]).then_inc(S.st, 16)
     g.sync.wait_ge(S.st, 16)
     g.wait_ge(S.sent, 2 * ne)

from concourse.bass import DstId, RemoteDMATransfer

NR = 8
F = 32

SCRATCH = {
    "xs": ("sbuf", [128, 128], "bfloat16"),
    "xq": ("sbuf", [128, 128], "bfloat16"),
    "ws": ("sbuf", [128, F], "bfloat16"),
    "gs": ("sbuf", [128, 128], "bfloat16"),
    "gqs": ("sbuf", [128, 128], "bfloat16"),
    "land": ("sbuf", [128, NR * F], "bfloat16"),
    "seed": ("sbuf", [128, 129], "bfloat16"),
    "skew": ("dram", [129, 128], "bfloat16"),
    "ident": ("sbuf", [128, 128], "bfloat16"),
    "ys": ("sbuf", [128, F], "bfloat16"),
    "gp": ("psum", [128, 512], "float32"),
    "pp": ("psum", [128, 512], "float32"),
    "gq": ("psum", [128, 512], "float32"),
    "qq": ("psum", [128, 512], "float32"),
}
SEMAPHORES = ["ldx", "ldw", "fill", "sk", "idr", "mm", "cp", "xin", "sent", "st"] + ["a%d" % j for j in range(NR)]


def rank_program(g, core, T, topo):
    rank = T.rank_of(core)
    if rank is None:
        return
    S = T.sem
    chips = []
    for c in T.cores:
        if topo.chip(c) not in chips:
            chips.append(topo.chip(c))
    members = [[c for c in T.cores if topo.chip(c) == ch] for ch in chips]
    nc, m = len(chips), len(members[0])
    assert m == 2 and all(len(x) == m for x in members)
    a = chips.index(topo.chip(core))
    b = members[a].index(core)
    partner = members[a][1 - b]

    def hops(d):
        return max(1 if topo.mates(chips[i], chips[(i + d) % nc]) or topo.same_plane(chips[i], chips[(i + d) % nc])
                   else 2 for i in range(nc))

    steps = [(d, e) for d in sorted(range(1, nc), key=lambda d: -hops(d)) for e in range(m)]
    dests = [members[(a + d) % nc][(b + e) % m] for d, e in steps]
    senders = [T.rank_of(members[(a - d) % nc][(b - e) % m]) for d, e in steps]
    mask = topo.mask(core, partner)
    for d in dests + [partner]:
        assert topo.may_write(core, d)
        mask &= topo.mask(core, d)
    ne = bin(mask).count("1")

    g.sync.dma_start(T.xs[:], T.x[:]).then_inc(S.ldx, 16)
    g.sync.dma_start(T.ws[:], T.w[:]).then_inc(S.ldw, 16)

    g.vector.memset(T.seed[:], 0.0).then_inc(S.fill, 1)
    g.vector.wait_ge(S.fill, 1)
    g.vector.memset(T.seed[:, 0:1], 1.0).then_inc(S.fill, 1)
    g.scalar.wait_ge(S.fill, 2)
    g.scalar.dma_start(T.skew[:], T.seed[:]).then_inc(S.sk, 16)
    g.scalar.wait_ge(S.sk, 16)
    g.scalar.dma_start(T.ident[:], T.skew[0:128, :]).then_inc(S.idr, 16)

    g.wait_ge(S.ldx, 16)
    rid, pid, _ = topo.addr(partner)
    g.remote_dma(T.xq[:], T.xs[:], remote_sem=S.xin, local_sem=S.sent, pid=pid, routing_id=rid, dma_engine_mask=mask)

    g.tensor.wait_ge(S.ldx, 16)
    g.tensor.matmul(T.gp[:, 0:128], T.xs[:], T.xs[:], start=True, stop=True).then_inc(S.mm, 1)
    g.vector.wait_ge(S.mm, 1)
    g.vector.tensor_copy(T.gs[:], T.gp[:, 0:128]).then_inc(S.cp, 1)
    g.tensor.wait_ge(S.cp, 1)
    g.tensor.wait_ge(S.ldw, 16)
    g.tensor.matmul(T.pp[:, 0:F], T.gs[:], T.ws[:], start=True, stop=True).then_inc(S.mm, 1)
    own = T.land[:, rank * F:(rank + 1) * F]
    g.vector.wait_ge(S.mm, 2)
    g.vector.tensor_copy(own, T.pp[:, 0:F]).then_inc(S.cp, 1)

    g.wait_ge(S.cp, 2)
    ids = []
    for d in dests:
        rid, pid, _ = topo.addr(d)
        ids.append(DstId(rid=rid, pnc=pid))
    g.remote_dma_fused(
        [RemoteDMATransfer(dst_ids=ids, dma_engine_mask=mask, remote_sem=S["a%d" % rank],
                           srcs=[own], dsts=[own for _ in dests])],
        local_sem=S.sent)

    yp = T.qq[:, 0:F]
    g.tensor.matmul(yp, T.gs[:], T.ws[:], start=True, stop=False)
    g.tensor.wait_ge(S.xin, ne)
    g.tensor.matmul(T.gq[:, 0:128], T.xq[:], T.xq[:], start=True, stop=True).then_inc(S.mm, 1)
    g.vector.wait_ge(S.mm, 3)
    g.vector.tensor_copy(T.gqs[:], T.gq[:, 0:128]).then_inc(S.cp, 1)
    g.tensor.wait_ge(S.idr, 16)
    late = len(senders) - 2
    for k, j in enumerate(senders):
        if k == late:
            g.tensor.wait_ge(S.cp, 3)
            g.tensor.matmul(yp, T.gqs[:], T.ws[:], start=False, stop=False)
        g.tensor.wait_ge(S["a%d" % j], ne)
        mmk = g.tensor.matmul(yp, T.ident[:], T.land[:, j * F:(j + 1) * F], start=False, stop=(k == len(senders) - 1))
    mmk.then_inc(S.mm, 1)

    g.vector.wait_ge(S.mm, 4)
    g.vector.tensor_copy(T.ys[:], yp).then_inc(S.cp, 1)
    g.sync.wait_ge(S.cp, 4)
    g.sync.dma_start(T.y[:], T.ys[:]).then_inc(S.st, 16)
    g.sync.wait_ge(S.st, 16)
    g.wait_ge(S.sent, 2 * ne)
